import numpy as np
import ml_dtypes


def mxq(x, axis, fmt="e4m3"):
    dtype, down = {"e4m3": (ml_dtypes.float8_e4m3fn, 7), "e5m2": (ml_dtypes.float8_e5m2, 14)}[fmt]
    v = np.moveaxis(np.asarray(x, np.float32).astype(ml_dtypes.bfloat16).astype(np.float64), axis, -1)
    blocks = v.reshape(v.shape[:-1] + (-1, 32))
    amax = np.abs(blocks).max(-1, keepdims=True)
    byte = np.maximum(np.where(amax > 0, np.frexp(amax)[1] - 1 + 127, 0) - down, 1)
    scale = np.exp2(byte - 127.0)
    codes = (blocks / scale).astype(np.float32).astype(dtype).astype(np.float64)
    return np.moveaxis((codes * scale).reshape(v.shape), -1, axis)


WIDE = False


def mx_kscale(k):
    if not WIDE:
        return np.ones(k)
    levels = np.array([10, -10, 5, -5, 0])
    if k % 512:
        return np.exp2(np.random.permutation(np.resize(levels, k // 32))).repeat(32)
    a = np.empty((k // 512, 16))
    for p in range(k // 512):
        a[p, :8] = np.random.permutation(np.resize(levels, 8))
        for g in range(8):
            far = levels[np.abs(levels - a[p, g]) >= 10]
            a[p, g + 8] = far[np.random.randint(len(far))]
    return np.exp2(a.ravel()).repeat(32)


BF16 = ml_dtypes.bfloat16


def bf(x):
    return np.asarray(x, np.float32).astype(BF16)


def f64(x):
    return np.asarray(x).astype(np.float64)


E2M1 = np.array([0.0, 0.5, 1.0, 1.5, 2.0, 3.0, 4.0, 6.0, -0.0, -0.5, -1.0, -1.5, -2.0, -3.0, -4.0, -6.0])


def pack_weight(w, fmt):
    k, n = w.shape
    w = f64(bf(w)).reshape(k // 32, 32, n)
    amax = np.abs(w).max(1)
    if fmt == "e4m3":
        byte = np.frexp(amax)[1] - 1 + 127 - 7
    else:
        mant, ex = np.frexp(amax / 6.0)
        byte = np.where(mant > 0.5, ex, ex - 1) + 127
    byte = np.clip(np.where(amax > 0, byte, 1), 1, 254)
    scaled = (w * np.exp2(127.0 - byte)[:, None, :]).reshape(k, n).astype(np.float32)
    by_word = np.ascontiguousarray(scaled.reshape(k // 512, 128, 4, n).transpose(0, 1, 3, 2))
    if fmt == "e4m3":
        words = by_word.astype(ml_dtypes.float8_e4m3fn).view(np.uint8)
    else:
        c = by_word.astype(ml_dtypes.float4_e2m1fn).view(np.uint8) & 0xF
        words = c[..., 0::2] | (c[..., 1::2] << 4)
    return np.ascontiguousarray(words), np.ascontiguousarray(byte.astype(np.uint8).reshape(k // 512, 16, n))


def unpack_weight(words, scales, fmt):
    g, p, n, _ = words.shape
    if fmt == "e4m3":
        vals = np.ascontiguousarray(words).view(ml_dtypes.float8_e4m3fn).astype(np.float64)
    else:
        nib = np.empty((g, p, n, 4), np.uint8)
        nib[..., 0::2] = words & 0xF
        nib[..., 1::2] = words >> 4
        vals = E2M1[nib]
    vals = vals * np.repeat(np.exp2(scales.astype(np.float64) - 127.0), 8, axis=1)[..., None]
    return vals.transpose(0, 1, 3, 2).reshape(g * 512, n)


B, L, D, E = 256, 4, 512, 1024


def erf(a):
    c = np.clip(a, -6.0, 6.0)
    c2 = c * c
    term = c
    total = c
    for n in range(1, 150):
        term = term * (2.0 * c2 / (2.0 * n + 1.0))
        total = total + term
    v = 2.0 / np.sqrt(np.pi) * np.exp(-c2) * total
    return np.where(np.abs(a) <= 6.0, v, np.sign(a))


def gelu_erf(v):
    return 0.5 * v * (1.0 + erf(v / np.sqrt(2.0)))


def softplus(r):
    return np.maximum(r, 0.0) + np.log(1.0 + np.exp(-np.abs(r)))


def draw0():
    s1, s2 = mx_kscale(D), mx_kscale(D)
    t = mx_kscale(E)
    c = 1.0 / np.sqrt(D)
    x = bf(np.random.standard_normal((B, L, D)) * s1)
    y = bf(np.random.standard_normal((B, D)) * s2)
    wu_words, wu_scales = pack_weight(np.random.standard_normal((D, E)) * c / s1[:, None] * t[None, :], "e4m3")
    bu = bf(np.random.standard_normal(E) * 0.3 * t)
    wg_words, wg_scales = pack_weight(np.random.standard_normal((D, E)) * c / s2[:, None], "e4m3")
    bg = bf(np.random.standard_normal(E) * 0.3)
    gain = bf((1.0 + 0.1 * np.random.standard_normal(E)) / t)
    return {
        "x": x,
        "y": y,
        "wu_words": wu_words,
        "wu_scales": wu_scales,
        "bu": bu,
        "wg_words": wg_words,
        "wg_scales": wg_scales,
        "bg": bg,
        "gain": gain,
    }


def core(x, y, wu_words, wu_scales, bu, wg_words, wg_scales, bg, gain):
    n, patches, _ = x.shape
    u = (mxq(f64(x), 2, "e4m3") @ unpack_weight(wu_words, wu_scales, "e4m3")) + f64(bu)
    g = f64(gain) * gelu_erf((mxq(f64(y), 1, "e4m3") @ unpack_weight(wg_words, wg_scales, "e4m3")) + f64(bg))
    u_flat = u.reshape(n * patches, u.shape[-1])
    s = (mxq(g, 1, "e4m3") @ mxq(u_flat, 1, "e4m3").T) / 16.0
    s = s.reshape(n, n, patches)
    idx = np.arange(n)
    positive = (idx[:, None] == idx[None, :])[:, :, None]
    r = np.where(positive, -s, s)
    return softplus(r)


def e4m3fn_bytes(y):
    return np.clip(np.asarray(y, np.float64), -448.0, 448.0).astype(np.float32).astype(ml_dtypes.float8_e4m3fn).view(np.uint8)


def e4m3fn_values(b):
    return np.asarray(b, np.uint8).view(ml_dtypes.float8_e4m3fn).astype(np.float64)


def setup_inputs():
    d = draw0()
    x0 = np.asarray(d['x']).astype(np.float64)
    s = (np.max(np.abs(x0), axis=(0, 1), keepdims=True) / 448.0).astype(np.float32)
    out = {}
    for k, v in d.items():
        if k == 'x':
            out['x_bytes'] = e4m3fn_bytes(x0 / s.astype(np.float64))
            out['x_scale'] = s
        else:
            out[k] = v
    return out


def reference(x_bytes, x_scale, y, wu_words, wu_scales, bu, wg_words, wg_scales, bg, gain):
    return core(e4m3fn_values(x_bytes) * x_scale.astype(np.float64), y, wu_words, wu_scales, bu, wg_words, wg_scales, bg, gain)

@@ -1,0 +1,428 @@
+from contextlib import ExitStack
+
+import concourse.mybir as mybir
+from concourse.masks import make_identity
+
+P = 128
+B, L, D, E = 256, 4, 512, 1024
+FLOPS = 2 * B * L * D * E + 2 * B * D * E + 2 * B * B * L * E
+
+F32 = mybir.dt.float32
+BF16 = mybir.dt.bfloat16
+I32 = mybir.dt.int32
+U32 = mybir.dt.uint32
+U8 = mybir.dt.uint8
+FP8 = mybir.dt.float8_e4m3fn
+X4 = mybir.dt.float8_e4m3fn_x4
+ALU = mybir.AluOpType
+ACT = mybir.ActivationFunctionType
+
+NC = 4
+CW = 256
+A = 64
+
+
+def tile_deepinfomaxlocalglobaljsdmap_w8_kernel(
+    tc, x_bytes, x_scale, y, wu_words, wu_scales, bu, wg_words, wg_scales, bg, gain, out
+):
+    nc = tc.nc
+    with ExitStack() as ctx:
+        keep = ctx.enter_context(tc.tile_pool(name="keep", bufs=1))
+        stage = ctx.enter_context(tc.tile_pool(name="stage", bufs=3))
+        ps_tr = ctx.enter_context(tc.psum_pool(name="ps_tr", bufs=2))
+        ps_a = ctx.enter_context(tc.psum_pool(name="ps_a", bufs=2))
+        ps_b = ctx.enter_context(tc.psum_pool(name="ps_b", bufs=2))
+        ps_s = ctx.enter_context(tc.psum_pool(name="ps_s", bufs=2))
+        ctx.enter_context(tc.manual_schedule())
+
+        xb0 = [keep.tile([P, 2, D], U8, name="xb%d" % c, align_bytes=A) for c in range(2)]
+        xb1 = keep.tile([P, 4, D], U8, name="xbh", align_bytes=A)
+        xsc = keep.tile([P, 4], F32, name="xsc", align_bytes=A)
+        yb = keep.tile([P, 2, D], BF16, name="yb", align_bytes=A)
+        w_raw = [keep.tile([P, E], I32, name="wraw%d" % w, align_bytes=A) for w in range(2)]
+        w_per = [keep.tile([P, E], I32, name="wper%d" % w, align_bytes=A) for w in range(2)]
+        sc_raw = [keep.tile([P, E // 4], I32, name="sraw%d" % w, align_bytes=A) for w in range(2)]
+        sc_per = [keep.tile([P, E // 4], I32, name="sper%d" % w, align_bytes=A) for w in range(2)]
+        rows_u = keep.tile([P, P], BF16, name="rows_u", align_bytes=A)
+        rows_g = keep.tile([P, P], BF16, name="rows_g", align_bytes=A)
+        ident = keep.tile([P, P], F32, name="ident", align_bytes=A)
+        ident_b = keep.tile([P, P], BF16, name="identb", align_bytes=A)
+        sgn = keep.tile([P, 4, P], F32, name="sgn", align_bytes=A)
+        ucols = keep.tile([P, 8], F32, name="ucols", align_bytes=A)
+        bgcols = keep.tile([P, 8], F32, name="bgcols", align_bytes=A)
+        gcols = keep.tile([P, 8], F32, name="gcols", align_bytes=A)
+        dummy = keep.tile([P, 2], F32, name="dummy", align_bytes=A)
+
+        def load_scales(w, src):
+            for q in range(4):
+                nc.sync.dma_start(out=sc_raw[w][32 * q : 32 * q + 4, :], in_=src[0, 4 * q : 4 * q + 4, :].bitcast(I32))
+
+        def load_vec(eng, rows, r0, vec):
+            eng.dma_start(out=rows[r0 : r0 + 8, :].rearrange("q (b i) -> q b i", i=8), in_=vec.rearrange("(b q i) -> q b i", q=8, i=8))
+
+        def load_w(w, src):
+            nc.sync.dma_start(out=w_raw[w][:], in_=src[0].rearrange("p n t -> p (n t)").bitcast(I32))
+
+        nc.vector.memset(sc_raw[0][:], 0)
+        nc.vector.memset(rows_u[:], 0.0)
+        nc.vector.memset(sc_raw[1][:], 0)
+        nc.vector.memset(rows_g[:], 0.0)
+        nc.vector.memset(dummy[:], 0.0)
+        nc.scalar.activation(dummy[:, 0:1], dummy[:, 1:2], ACT.Gelu)
+        nc.sync.dma_start(out=xb0[0][:], in_=x_bytes[0:P, 0:2, :])
+        nc.sync.dma_start(out=xsc[:], in_=x_scale.rearrange("a b (p t) -> p (a b t)", t=4))
+        load_scales(0, wu_scales)
+        nc.sync.dma_start(out=xb0[1][:], in_=x_bytes[0:P, 2:4, :])
+        load_w(0, wu_words)
+        nc.sync.dma_start(out=xb1[:], in_=x_bytes[P : 2 * P, :, :])
+        load_vec(nc.sync, rows_u, 0, bu)
+        load_scales(1, wg_scales)
+        load_w(1, wg_words)
+        make_identity(nc, ident[:])
+        nc.gpsimd.dma_start(out=yb[:], in_=y.rearrange("(n p) k -> p n k", p=P))
+        load_vec(nc.gpsimd, rows_g, 0, bg)
+        load_vec(nc.gpsimd, rows_g, 8, gain)
+        nc.vector.tensor_copy(out=ident_b[:], in_=ident[:])
+        nc.vector.tensor_scalar(
+            out=sgn[:], in0=ident[:].unsqueeze(1).to_broadcast([P, 4, P]), scalar1=-2.0, scalar2=1.0, op0=ALU.mult, op1=ALU.add
+        )
+
+        xw, xtr, xg, xc, xs = {}, {}, {}, {}, {}
+
+        def cast(c, n, eng):
+            if c not in xw:
+                xw[c] = keep.tile([P, 2, D], BF16, name="xw%d" % c, align_bytes=A)
+            src = (xb0[c][:, n, :] if c < 2 else xb1[:, 2 * (c - 2) + n, :]).bitcast(FP8)
+            if eng == "V":
+                nc.vector.tensor_copy(out=xw[c][:, n, :], in_=src)
+            elif eng == "G":
+                nc.gpsimd.tensor_copy(out=xw[c][:, n, :], in_=src)
+            else:
+                nc.scalar.copy(out=xw[c][:, n, :], in_=src)
+
+        def transposes(src_tile, tr, n):
+            words = src_tile[:, n, :].bitcast(F32)
+            for u in range(2):
+                nc.tensor.transpose(tr[:, u, P * n : P * n + P], words[:, u : D // 2 : 2], ident[:])
+
+        def xtrn(c, n):
+            if n == 0:
+                xtr[c] = ps_tr.tile([P, 2, CW], F32, name="tr")
+            transposes(xw[c], xtr[c], n)
+
+        def xtt(c):
+            xg[c] = keep.tile([P, 4 * CW], BF16, name="xg%d" % c, align_bytes=A)
+            flat = xtr[c][:].rearrange("p u r -> p (u r)").bitcast(BF16)
+            nc.vector.tensor_tensor(
+                out=xg[c][:].rearrange("p (r u e) -> p r u e", u=2, e=2),
+                in0=flat.rearrange("p (u r e) -> p r u e", u=2, e=2),
+                in1=xsc[:].rearrange("p (u e) -> p u e", u=2).unsqueeze(1).to_broadcast([P, CW, 2, 2]),
+                op=ALU.mult,
+            )
+
+        def quant(src, name):
+            codes = keep.tile([P, CW], U32, name=name + "c", align_bytes=A)
+            plane = keep.tile([P, CW], U8, name=name + "s", align_bytes=A)
+            nc.vector.quantize_mx(out=codes[:].bitcast(X4), scales=plane[:], in_=src[:])
+            return codes, plane
+
+        def xq(c):
+            xc[c], xs[c] = quant(xg[c], "x%d" % c)
+
+        def perm(w):
+            nc.vector.tensor_copy(
+                out=sc_per[w][:].rearrange("p (q b i) -> p q b i", q=8, i=2),
+                in_=sc_raw[w][:].rearrange("p (b q i) -> p q b i", q=8, i=2),
+            )
+            nc.vector.tensor_copy(
+                out=w_per[w][:].rearrange("p (q b i) -> p q b i", q=8, i=8),
+                in_=w_raw[w][:].rearrange("p (b q i) -> p q b i", q=8, i=8),
+            )
+
+        def weights(w, g, t):
+            c0 = P * (4 * g + t)
+            return w_per[w][:, c0 : c0 + P].bitcast(X4), sc_per[w][:].bitcast(U8)[:, c0 : c0 + P]
+
+        bt = {}
+
+        def btru():
+            bt[0] = ps_b.tile([P, P], BF16, name="pb")
+            nc.tensor.transpose(bt[0][:], rows_u[:], ident_b[:])
+
+        def bcpu():
+            nc.vector.tensor_copy(out=ucols[:], in_=bt[0][:, 0:8])
+
+        def btrg():
+            bt[1] = ps_b.tile([P, P], BF16, name="pb")
+            nc.tensor.transpose(bt[1][:], rows_g[:], ident_b[:])
+
+        def bcpg():
+            nc.vector.tensor_copy(out=bgcols[:], in_=bt[1][:, 0:8])
+            nc.vector.tensor_scalar(out=gcols[:], in0=bt[1][:, 8:16], scalar1=0.0625, scalar2=None, op0=ALU.mult)
+
+        up, ub, ug, uc, us = {}, {}, {}, {}, {}
+
+        def umm_v(c, g, n):
+            up[c, g, n] = ps_a.tile([P, 4, P], F32, name="pa")
+            for t in range(4):
+                lw, ls = weights(0, g, t)
+                nc.tensor.matmul_mx(
+                    out=up[c, g, n][:, t, :], lhsT=lw, lhsT_scale=ls,
+                    rhs=xc[c][:, P * n : P * n + P].bitcast(X4), rhs_scale=xs[c][:, P * n : P * n + P],
+                    start=True, stop=True,
+                )
+
+        def get_ug(c, g):
+            if (c, g) not in ug:
+                ug[c, g] = keep.tile([P, 4 * CW], BF16, name="ug%d%d" % (c, g), align_bytes=A)
+            return ug[c, g]
+
+        def utt(c, g, n):
+            nc.vector.tensor_tensor(
+                out=get_ug(c, g)[:, 512 * n : 512 * n + 512].rearrange("p (r t) -> p r t", t=4),
+                in0=up[c, g, n][:].rearrange("p t r -> p r t"),
+                in1=ucols[:, 4 * g : 4 * g + 4].unsqueeze(1).to_broadcast([P, P, 4]),
+                op=ALU.add,
+            )
+
+        def umm_s(c, g, k):
+            up[c, g, k] = ps_b.tile([P, 2, CW], F32, name="pb")
+            for j in range(2):
+                lw, ls = weights(0, g, 2 * k + j)
+                nc.tensor.matmul_mx(
+                    out=up[c, g, k][:, j, :], lhsT=lw, lhsT_scale=ls,
+                    rhs=xc[c][:].bitcast(X4), rhs_scale=xs[c][:], start=True, stop=True,
+                )
+
+        def uact(c, g, k):
+            if (c, g) not in ub:
+                ub[c, g] = keep.tile([P, 4, CW], BF16, name="ub%d%d" % (c, g), align_bytes=A)
+            for j in range(2):
+                t = 2 * k + j
+                nc.scalar.activation(ub[c, g][:, t, :], up[c, g, k][:, j, :], ACT.Identity, bias=ucols[:, 4 * g + t : 4 * g + t + 1])
+
+        def uil(c, g, n, eng):
+            o = get_ug(c, g)[:, 512 * n : 512 * n + 512].rearrange("p (r t) -> p r t", t=4)
+            i = ub[c, g][:, :, P * n : P * n + P].rearrange("p t r -> p r t")
+            if eng == "G":
+                nc.gpsimd.tensor_scalar(out=o, in0=i, scalar1=1.0, scalar2=0.0, op0=ALU.mult, op1=ALU.add)
+            else:
+                nc.vector.tensor_copy(out=o, in_=i)
+
+        def uq(c, g):
+            uc[c, g], us[c, g] = quant(ug[c, g], "u%d%d" % (c, g))
+
+        gp, gel, gg, gc, gs = {}, {}, {}, {}, {}
+        yt, ygt, yq_ = {}, {}, {}
+
+        def ytr():
+            yt[0] = ps_tr.tile([P, 2, CW], F32, name="tr")
+            for n in range(2):
+                transposes(yb, yt[0], n)
+
+        def ycp():
+            ygt[0] = keep.tile([P, 4 * CW], BF16, name="yg", align_bytes=A)
+            nc.scalar.copy(out=ygt[0][:].bitcast(F32).rearrange("p (r u) -> p r u", u=2), in_=yt[0][:].rearrange("p u r -> p r u"))
+
+        def yq():
+            yq_[0], yq_[1] = quant(ygt[0], "y")
+
+        def gmm(g, k):
+            gp[g, k] = ps_b.tile([P, 2, CW], F32, name="pb")
+            for j in range(2):
+                lw, ls = weights(1, g, 2 * k + j)
+                nc.tensor.matmul_mx(
+                    out=gp[g, k][:, j, :], lhsT=lw, lhsT_scale=ls,
+                    rhs=yq_[0][:].bitcast(X4), rhs_scale=yq_[1][:], start=True, stop=True,
+                )
+
+        def gelu(g, k):
+            if g not in gel:
+                gel[g] = keep.tile([P, 4, CW], F32, name="gel%d" % g, align_bytes=A)
+            for j in range(2):
+                t = 2 * k + j
+                nc.scalar.activation(gel[g][:, t, :], gp[g, k][:, j, :], ACT.Gelu, bias=bgcols[:, 4 * g + t : 4 * g + t + 1])
+
+        def gmul(g, n, eng):
+            if g not in gg:
+                gg[g] = keep.tile([P, 4 * CW], BF16, name="gg%d" % g, align_bytes=A)
+            e = nc.gpsimd if eng == "G" else nc.vector
+            e.tensor_tensor(
+                out=gg[g][:, 512 * n : 512 * n + 512].rearrange("p (r t) -> p r t", t=4),
+                in0=gel[g][:, :, P * n : P * n + P].rearrange("p t r -> p r t"),
+                in1=gcols[:, 4 * g : 4 * g + 4].unsqueeze(1).to_broadcast([P, P, 4]),
+                op=ALU.mult,
+            )
+
+        def gq(g):
+            gc[g], gs[g] = quant(gg[g], "g%d" % g)
+
+        sp, rt, ex, wt = {}, {}, {}, {}
+
+        def smm(c, i):
+            h, lp = c // 2, c % 2
+            if lp == 0:
+                sp[h, i] = ps_s.tile([P, 512], F32, name="s") if h == 0 else ps_tr.tile([P, 512], F32, name="tr")
+            for g in range(2):
+                nc.tensor.matmul_mx(
+                    out=sp[h, i][:, CW * lp : CW * lp + CW],
+                    lhsT=gc[g][:, P * i : P * i + P].bitcast(X4), lhsT_scale=gs[g][:, P * i : P * i + P],
+                    rhs=uc[c, g][:].bitcast(X4), rhs_scale=us[c, g][:],
+                    start=(g == 0), stop=(g == 1),
+                )
+
+        def diag(c):
+            h, lp = c // 2, c % 2
+            cs = slice(CW * lp, CW * lp + CW)
+            if h not in rt:
+                rt[h] = keep.tile([P, 512], F32, name="rt%d" % h, align_bytes=A)
+            nc.vector.tensor_tensor(
+                out=rt[h][:, cs].rearrange("p (l j) -> p l j", l=2), in0=sp[h, h][:, cs].rearrange("p (l j) -> p l j", l=2),
+                in1=sgn[:, 2 * lp : 2 * lp + 2, :], op=ALU.mult,
+            )
+
+        def exp(c, i):
+            h, lp = c // 2, c % 2
+            cs = slice(CW * lp, CW * lp + CW)
+            if (h, i) not in ex:
+                ex[h, i] = keep.tile([P, 512], F32, name="ex%d%d" % (h, i), align_bytes=A)
+            src = rt[h][:, cs] if i == h else sp[h, i][:, cs]
+            nc.scalar.activation(ex[h, i][:, cs], src, ACT.Exp)
+
+        def ln(h, i):
+            wt[h, i] = keep.tile([P, 512], F32, name="w%d%d" % (h, i), align_bytes=A)
+            nc.scalar.activation(wt[h, i][:], ex[h, i][:], ACT.Ln, bias=1.0)
+
+        def stt(h, i):
+            o = keep.tile([P, 512], F32, name="o%d%d" % (h, i), align_bytes=A)
+            r = rt[h] if i == h else sp[h, i]
+            nc.vector.scalar_tensor_tensor(
+                out=o[:].rearrange("p (j l) -> p j l", l=4),
+                in0=wt[h, i][:].rearrange("p (l j) -> p j l", l=4), scalar=44.0,
+                in1=r[:].rearrange("p (l j) -> p j l", l=4), op0=ALU.min, op1=ALU.max,
+            )
+            nc.sync.dma_start(out=out[P * i : P * i + P, P * h : P * h + P, :].rearrange("i j l -> i (j l)"), in_=o[:])
+
+        cast(0, 0, "V")
+        cast(0, 1, "S")
+        xtrn(0, 0)
+        cast(1, 1, "S")
+        xtrn(0, 1)
+        perm(0)
+        cast(1, 0, "S")
+        xtt(0)
+        xtrn(1, 0)
+        xtrn(1, 1)
+        btru()
+        cast(2, 1, "S")
+        bcpu()
+        ytr()
+        xtt(1)
+        cast(2, 0, "S")
+        ycp()
+        perm(1)
+        xtrn(2, 0)
+        xtrn(2, 1)
+        cast(3, 1, "S")
+        btrg()
+        yq()
+        cast(3, 0, "S")
+        bcpg()
+        gmm(0, 1)
+        xtt(2)
+        gmm(0, 0)
+        gelu(0, 1)
+        xtrn(3, 0)
+        xtrn(3, 1)
+        gelu(0, 0)
+        gmm(1, 0)
+        xtt(3)
+        gelu(1, 0)
+        gmm(1, 1)
+        gmul(0, 0, "G")
+        xq(0)
+        gelu(1, 1)
+        xq(3)
+        umm_v(0, 0, 1)
+        xq(1)
+        gmul(0, 1, "G")
+        umm_s(3, 1, 1)
+        utt(0, 0, 1)
+        umm_s(3, 1, 0)
+        uact(3, 1, 1)
+        umm_v(3, 0, 1)
+        xq(2)
+        umm_v(3, 0, 0)
+        gmul(1, 1, "G")
+        uact(3, 1, 0)
+        gq(0)
+        umm_s(1, 1, 1)
+        utt(3, 0, 1)
+        uact(1, 1, 1)
+        umm_s(2, 1, 0)
+        utt(3, 0, 0)
+        umm_v(2, 0, 1)
+        gmul(1, 0, "G")
+        uact(2, 1, 0)
+        umm_s(2, 1, 1)
+        utt(2, 0, 1)
+        umm_v(2, 0, 0)
+        uact(2, 1, 1)
+        umm_s(0, 1, 0)
+        utt(2, 0, 0)
+        uil(3, 1, 0, "G")
+        umm_v(1, 0, 0)
+        uact(0, 1, 0)
+        gq(1)
+        umm_s(1, 1, 0)
+        uil(2, 1, 0, "G")
+        umm_v(1, 0, 1)
+        uq(2, 0)
+        uact(1, 1, 0)
+        uq(3, 0)
+        umm_s(0, 1, 1)
+        uil(2, 1, 1, "G")
+        utt(1, 0, 1)
+        uact(0, 1, 1)
+        uil(1, 1, 1, "G")
+        uq(2, 1)
+        umm_v(0, 0, 0)
+        utt(1, 0, 0)
+        smm(2, 0)
+        uil(0, 1, 0, "G")
+        smm(2, 1)
+        exp(2, 0)
+        utt(0, 0, 0)
+        uil(0, 1, 1, "G")
+        uq(1, 0)
+        uq(0, 0)
+        uil(3, 1, 1, "G")
+        uq(0, 1)
+        diag(2)
+        smm(0, 1)
+        uil(1, 1, 0, "G")
+        uq(3, 1)
+        smm(0, 0)
+        exp(2, 1)
+        smm(3, 0)
+        exp(0, 1)
+        diag(0)
+        smm(3, 1)
+        uq(1, 1)
+        exp(3, 0)
+        diag(3)
+        exp(0, 0)
+        smm(1, 1)
+        smm(1, 0)
+        exp(3, 1)
+        exp(1, 1)
+        diag(1)
+        exp(1, 0)
+        ln(1, 0)
+        ln(0, 0)
+        stt(1, 0)
+        ln(1, 1)
+        stt(0, 0)
+        ln(0, 1)
+        stt(1, 1)
+        stt(0, 1)

@@ -75,11 +75,11 @@ def tile_deepinfomaxlocalglobaljsdmap_w8_kernel(
         nc.sync.dma_start(out=xb0[1][:], in_=x_bytes[0:P, 2:4, :])
         load_w(0, wu_words)
         nc.sync.dma_start(out=xb1[:], in_=x_bytes[P : 2 * P, :, :])
-        load_vec(nc.sync, rows_u, 0, bu)
-        load_scales(1, wg_scales)
+        nc.sync.dma_start(out=yb[:], in_=y.rearrange("(n p) k -> p n k", p=P))
         load_w(1, wg_words)
+        load_scales(1, wg_scales)
         make_identity(nc, ident[:])
-        nc.gpsimd.dma_start(out=yb[:], in_=y.rearrange("(n p) k -> p n k", p=P))
+        load_vec(nc.gpsimd, rows_u, 0, bu)
         load_vec(nc.gpsimd, rows_g, 0, bg)
         load_vec(nc.gpsimd, rows_g, 8, gain)
         nc.vector.tensor_copy(out=ident_b[:], in_=ident[:])
@@ -120,14 +120,33 @@ def tile_deepinfomaxlocalglobaljsdmap_w8_kernel(
                 op=ALU.mult,
             )
 
-        def quant(src, name):
-            codes = keep.tile([P, CW], U32, name=name + "c", align_bytes=A)
-            plane = keep.tile([P, CW], U8, name=name + "s", align_bytes=A)
-            nc.vector.quantize_mx(out=codes[:].bitcast(X4), scales=plane[:], in_=src[:])
+        def quant(src, name, width):
+            codes = keep.tile([P, width], U32, name=name + "c", align_bytes=A)
+            plane = keep.tile([P, width], U8, name=name + "s", align_bytes=A)
+            nc.vector.quantize_mx(out=codes[:].bitcast(X4), scales=plane[:], in_=src)
             return codes, plane
 
+        def xst():
+            xtr["s"] = ps_tr.tile([P, 4, P], F32, name="tr")
+            for t in range(4):
+                nc.tensor.transpose(xtr["s"][:, t, :], xsc[:, t : t + 1].to_broadcast([P, P]), ident[:])
+
+        def xscp():
+            xg["s"] = keep.tile([P, D], F32, name="xsb", align_bytes=A)
+            nc.scalar.copy(out=xg["s"][:].rearrange("p (k t) -> p k t", t=4), in_=xtr["s"][:].rearrange("p t k -> p k t"))
+
+        def xtt2(c, n):
+            if c not in xw:
+                xw[c] = keep.tile([P, 2, D], BF16, name="xw%d" % c, align_bytes=A)
+            src = (xb0[c][:, n, :] if c < 2 else xb1[:, 2 * (c - 2) + n, :]).bitcast(FP8)
+            nc.vector.tensor_tensor(out=xw[c][:, n, :], in0=src, in1=xg["s"][:], op=ALU.mult)
+
+        def xcp(c):
+            xg[c] = keep.tile([P, 4 * CW], BF16, name="xg%d" % c, align_bytes=A)
+            nc.scalar.copy(out=xg[c][:].bitcast(F32).rearrange("p (r u) -> p r u", u=2), in_=xtr[c][:].rearrange("p u r -> p r u"))
+
         def xq(c):
-            xc[c], xs[c] = quant(xg[c], "x%d" % c)
+            xc[c], xs[c] = quant(xg[c][:], "x%d" % c, CW)
 
         def perm(w):
             nc.vector.tensor_copy(
@@ -173,9 +192,9 @@ def tile_deepinfomaxlocalglobaljsdmap_w8_kernel(
                 )
 
         def get_ug(c, g):
-            if (c, g) not in ug:
-                ug[c, g] = keep.tile([P, 4 * CW], BF16, name="ug%d%d" % (c, g), align_bytes=A)
-            return ug[c, g]
+            if c not in ug:
+                ug[c] = keep.tile([P, 2, 4 * CW], BF16, name="ug%d" % c, align_bytes=A)
+            return ug[c][:, g, :]
 
         def utt(c, g, n):
             nc.vector.tensor_tensor(
@@ -206,11 +225,13 @@ def tile_deepinfomaxlocalglobaljsdmap_w8_kernel(
             i = ub[c, g][:, :, P * n : P * n + P].rearrange("p t r -> p r t")
             if eng == "G":
                 nc.gpsimd.tensor_scalar(out=o, in0=i, scalar1=1.0, scalar2=0.0, op0=ALU.mult, op1=ALU.add)
+            elif eng == "S":
+                nc.scalar.copy(out=o, in_=i)
             else:
                 nc.vector.tensor_copy(out=o, in_=i)
 
-        def uq(c, g):
-            uc[c, g], us[c, g] = quant(ug[c, g], "u%d%d" % (c, g))
+        def uq(c):
+            uc[c], us[c] = quant(ug[c][:].rearrange("p g n -> p (g n)"), "u%d" % c, 2 * CW)
 
         gp, gel, gg, gc, gs = {}, {}, {}, {}, {}
         yt, ygt, yq_ = {}, {}, {}
@@ -225,7 +246,7 @@ def tile_deepinfomaxlocalglobaljsdmap_w8_kernel(
             nc.scalar.copy(out=ygt[0][:].bitcast(F32).rearrange("p (r u) -> p r u", u=2), in_=yt[0][:].rearrange("p u r -> p r u"))
 
         def yq():
-            yq_[0], yq_[1] = quant(ygt[0], "y")
+            yq_[0], yq_[1] = quant(ygt[0][:], "y", CW)
 
         def gmm(g, k):
             gp[g, k] = ps_b.tile([P, 2, CW], F32, name="pb")
@@ -244,18 +265,18 @@ def tile_deepinfomaxlocalglobaljsdmap_w8_kernel(
                 nc.scalar.activation(gel[g][:, t, :], gp[g, k][:, j, :], ACT.Gelu, bias=bgcols[:, 4 * g + t : 4 * g + t + 1])
 
         def gmul(g, n, eng):
-            if g not in gg:
-                gg[g] = keep.tile([P, 4 * CW], BF16, name="gg%d" % g, align_bytes=A)
+            if 0 not in gg:
+                gg[0] = keep.tile([P, 2, 4 * CW], BF16, name="gg", align_bytes=A)
             e = nc.gpsimd if eng == "G" else nc.vector
             e.tensor_tensor(
-                out=gg[g][:, 512 * n : 512 * n + 512].rearrange("p (r t) -> p r t", t=4),
+                out=gg[0][:, g, 512 * n : 512 * n + 512].rearrange("p (r t) -> p r t", t=4),
                 in0=gel[g][:, :, P * n : P * n + P].rearrange("p t r -> p r t"),
                 in1=gcols[:, 4 * g : 4 * g + 4].unsqueeze(1).to_broadcast([P, P, 4]),
                 op=ALU.mult,
             )
 
-        def gq(g):
-            gc[g], gs[g] = quant(gg[g], "g%d" % g)
+        def gq():
+            gc[0], gs[0] = quant(gg[0][:].rearrange("p g n -> p (g n)"), "g", 2 * CW)
 
         sp, rt, ex, wt = {}, {}, {}, {}
 
@@ -266,8 +287,8 @@ def tile_deepinfomaxlocalglobaljsdmap_w8_kernel(
             for g in range(2):
                 nc.tensor.matmul_mx(
                     out=sp[h, i][:, CW * lp : CW * lp + CW],
-                    lhsT=gc[g][:, P * i : P * i + P].bitcast(X4), lhsT_scale=gs[g][:, P * i : P * i + P],
-                    rhs=uc[c, g][:].bitcast(X4), rhs_scale=us[c, g][:],
+                    lhsT=gc[0][:, CW * g + P * i : CW * g + P * i + P].bitcast(X4), lhsT_scale=gs[0][:, CW * g + P * i : CW * g + P * i + P],
+                    rhs=uc[c][:, CW * g : CW * g + CW].bitcast(X4), rhs_scale=us[c][:, CW * g : CW * g + CW],
                     start=(g == 0), stop=(g == 1),
                 )
 
@@ -308,121 +329,114 @@ def tile_deepinfomaxlocalglobaljsdmap_w8_kernel(
         xtrn(0, 0)
         cast(1, 1, "S")
         xtrn(0, 1)
-        perm(0)
-        cast(1, 0, "S")
         xtt(0)
+        cast(1, 0, "S")
         xtrn(1, 0)
         xtrn(1, 1)
+        perm(0)
         btru()
-        cast(2, 1, "S")
-        bcpu()
-        ytr()
-        xtt(1)
         cast(2, 0, "S")
+        xq(0)
+        ytr()
+        bcpu()
+        xtt(1)
+        cast(2, 1, "S")
+        umm_s(0, 1, 0)
+        umm_v(0, 0, 1)
         ycp()
+        umm_v(0, 0, 0)
         perm(1)
+        btrg()
+        uact(0, 1, 0)
         xtrn(2, 0)
         xtrn(2, 1)
-        cast(3, 1, "S")
-        btrg()
-        yq()
-        cast(3, 0, "S")
         bcpg()
-        gmm(0, 1)
+        cast(3, 1, "S")
+        umm_s(0, 1, 1)
         xtt(2)
-        gmm(0, 0)
-        gelu(0, 1)
-        xtrn(3, 0)
-        xtrn(3, 1)
-        gelu(0, 0)
-        gmm(1, 0)
-        xtt(3)
-        gelu(1, 0)
-        gmm(1, 1)
-        gmul(0, 0, "G")
-        xq(0)
-        gelu(1, 1)
-        xq(3)
-        umm_v(0, 0, 1)
+        uact(0, 1, 1)
+        cast(3, 0, "S")
+        yq()
         xq(1)
-        gmul(0, 1, "G")
-        umm_s(3, 1, 1)
-        utt(0, 0, 1)
-        umm_s(3, 1, 0)
-        uact(3, 1, 1)
-        umm_v(3, 0, 1)
+        gmm(1, 1)
         xq(2)
-        umm_v(3, 0, 0)
-        gmul(1, 1, "G")
-        uact(3, 1, 0)
-        gq(0)
-        umm_s(1, 1, 1)
-        utt(3, 0, 1)
-        uact(1, 1, 1)
-        umm_s(2, 1, 0)
-        utt(3, 0, 0)
-        umm_v(2, 0, 1)
+        gmm(1, 0)
+        gelu(1, 1)
+        xtrn(3, 0)
+        uil(0, 1, 0, "G")
+        utt(0, 0, 0)
+        xtrn(3, 1)
+        gelu(1, 0)
+        utt(0, 0, 1)
+        umm_s(1, 1, 0)
+        uil(0, 1, 1, "G")
+        umm_v(1, 0, 0)
+        xtt(3)
+        uact(1, 1, 0)
+        gmm(0, 0)
         gmul(1, 0, "G")
-        uact(2, 1, 0)
+        umm_v(2, 0, 0)
+        gelu(0, 0)
+        gmm(0, 1)
+        utt(1, 0, 0)
+        gmul(1, 1, "G")
+        gelu(0, 1)
+        umm_s(1, 1, 1)
+        utt(2, 0, 0)
+        umm_v(2, 0, 1)
+        uact(1, 1, 1)
         umm_s(2, 1, 1)
         utt(2, 0, 1)
-        umm_v(2, 0, 0)
-        uact(2, 1, 1)
-        umm_s(0, 1, 0)
-        utt(2, 0, 0)
-        uil(3, 1, 0, "G")
-        umm_v(1, 0, 0)
-        uact(0, 1, 0)
-        gq(1)
-        umm_s(1, 1, 0)
-        uil(2, 1, 0, "G")
         umm_v(1, 0, 1)
-        uq(2, 0)
-        uact(1, 1, 0)
-        uq(3, 0)
-        umm_s(0, 1, 1)
-        uil(2, 1, 1, "G")
+        gmul(0, 0, "G")
+        uact(2, 1, 1)
+        umm_s(2, 1, 0)
         utt(1, 0, 1)
-        uact(0, 1, 1)
-        uil(1, 1, 1, "G")
-        uq(2, 1)
-        umm_v(0, 0, 0)
-        utt(1, 0, 0)
+        uil(1, 1, 1, "S")
+        xq(3)
+        uq(0)
+        umm_v(3, 1, 1)
+        uact(2, 1, 0)
+        umm_v(3, 0, 0)
+        gmul(0, 1, "G")
+        utt(3, 1, 1)
+        uil(1, 1, 0, "S")
+        utt(3, 0, 0)
+        umm_v(3, 1, 0)
+        uil(2, 1, 1, "G")
+        utt(3, 1, 0)
+        umm_v(3, 0, 1)
+        gq()
+        uil(2, 1, 0, "G")
+        utt(3, 0, 1)
+        smm(0, 1)
+        smm(0, 0)
+        exp(0, 1)
+        uq(1)
+        uq(2)
+        smm(1, 0)
+        smm(1, 1)
+        uq(3)
         smm(2, 0)
-        uil(0, 1, 0, "G")
         smm(2, 1)
         exp(2, 0)
-        utt(0, 0, 0)
-        uil(0, 1, 1, "G")
-        uq(1, 0)
-        uq(0, 0)
-        uil(3, 1, 1, "G")
-        uq(0, 1)
-        diag(2)
-        smm(0, 1)
-        uil(1, 1, 0, "G")
-        uq(3, 1)
-        smm(0, 0)
-        exp(2, 1)
-        smm(3, 0)
-        exp(0, 1)
         diag(0)
         smm(3, 1)
-        uq(1, 1)
-        exp(3, 0)
-        diag(3)
-        exp(0, 0)
-        smm(1, 1)
-        smm(1, 0)
-        exp(3, 1)
         exp(1, 1)
+        smm(3, 0)
+        diag(2)
+        exp(0, 0)
+        diag(3)
+        exp(2, 1)
         diag(1)
+        exp(3, 0)
+        exp(3, 1)
         exp(1, 0)
-        ln(1, 0)
         ln(0, 0)
-        stt(1, 0)
         ln(1, 1)
         stt(0, 0)
-        ln(0, 1)
+        ln(1, 0)
         stt(1, 1)
+        ln(0, 1)
+        stt(1, 0)
         stt(0, 1)

@@ -69,19 +69,30 @@ def tile_deepinfomaxlocalglobaljsdmap_w8_kernel(
         nc.vector.memset(rows_g[:], 0.0)
         nc.vector.memset(dummy[:], 0.0)
         nc.scalar.activation(dummy[:, 0:1], dummy[:, 1:2], ACT.Gelu)
-        nc.sync.dma_start(out=xb0[0][:], in_=x_bytes[0:P, 0:2, :])
         nc.sync.dma_start(out=xsc[:], in_=x_scale.rearrange("a b (p t) -> p (a b t)", t=4))
+        nc.sync.dma_start(out=xb0[0][:], in_=x_bytes[0:P, 0:2, :])
         load_scales(0, wu_scales)
-        nc.sync.dma_start(out=xb0[1][:], in_=x_bytes[0:P, 2:4, :])
         load_w(0, wu_words)
+        nc.sync.dma_start(out=xb0[1][:], in_=x_bytes[0:P, 2:4, :])
+        load_vec(nc.sync, rows_u, 0, bu)
         nc.sync.dma_start(out=xb1[:], in_=x_bytes[P : 2 * P, :, :])
         nc.sync.dma_start(out=yb[:], in_=y.rearrange("(n p) k -> p n k", p=P))
         load_w(1, wg_words)
         load_scales(1, wg_scales)
+        load_vec(nc.sync, rows_g, 0, bg)
+        load_vec(nc.sync, rows_g, 8, gain)
         make_identity(nc, ident[:])
-        load_vec(nc.gpsimd, rows_u, 0, bu)
-        load_vec(nc.gpsimd, rows_g, 0, bg)
-        load_vec(nc.gpsimd, rows_g, 8, gain)
+
+        def warm(count):
+            wps = ps_a.tile([P, 512], F32, name="pa")
+            for i in range(count):
+                nc.tensor.matmul(wps[:], zeros[:, 0:P], zeros[:], start=True, stop=True)
+
+        zeros = keep.tile([P, 512], BF16, name="zeros", align_bytes=A)
+        nc.vector.memset(zeros[:], 0.0)
+        half = keep.tile([P, 1], F32, name="half", align_bytes=A)
+        nc.vector.memset(half[:], 0.5)
+        warm(4)
         nc.vector.tensor_copy(out=ident_b[:], in_=ident[:])
         nc.vector.tensor_scalar(
             out=sgn[:], in0=ident[:].unsqueeze(1).to_broadcast([P, 4, P]), scalar1=-2.0, scalar2=1.0, op0=ALU.mult, op1=ALU.add
@@ -169,15 +180,15 @@ def tile_deepinfomaxlocalglobaljsdmap_w8_kernel(
             nc.tensor.transpose(bt[0][:], rows_u[:], ident_b[:])
 
         def bcpu():
-            nc.vector.tensor_copy(out=ucols[:], in_=bt[0][:, 0:8])
+            nc.scalar.copy(out=ucols[:], in_=bt[0][:, 0:8])
 
         def btrg():
             bt[1] = ps_b.tile([P, P], BF16, name="pb")
             nc.tensor.transpose(bt[1][:], rows_g[:], ident_b[:])
 
         def bcpg():
-            nc.vector.tensor_copy(out=bgcols[:], in_=bt[1][:, 0:8])
-            nc.vector.tensor_scalar(out=gcols[:], in0=bt[1][:, 8:16], scalar1=0.0625, scalar2=None, op0=ALU.mult)
+            nc.scalar.copy(out=bgcols[:], in_=bt[1][:, 0:8])
+            nc.scalar.activation(gcols[:], bt[1][:, 8:16], ACT.Copy, scale=0.0625)
 
         up, ub, ug, uc, us = {}, {}, {}, {}, {}
 
@@ -220,18 +231,30 @@ def tile_deepinfomaxlocalglobaljsdmap_w8_kernel(
                 t = 2 * k + j
                 nc.scalar.activation(ub[c, g][:, t, :], up[c, g, k][:, j, :], ACT.Identity, bias=ucols[:, 4 * g + t : 4 * g + t + 1])
 
-        def uil(c, g, n, eng):
-            o = get_ug(c, g)[:, 512 * n : 512 * n + 512].rearrange("p (r t) -> p r t", t=4)
-            i = ub[c, g][:, :, P * n : P * n + P].rearrange("p t r -> p r t")
-            if eng == "G":
-                nc.gpsimd.tensor_scalar(out=o, in0=i, scalar1=1.0, scalar2=0.0, op0=ALU.mult, op1=ALU.add)
-            elif eng == "S":
+        def uil(c, g, eng):
+            o = get_ug(c, g).rearrange("p (r i t) -> p r t i", i=4, t=4)
+            i = ub[c, g][:].rearrange("p t (r i) -> p r t i", i=4)
+            if eng == "S":
                 nc.scalar.copy(out=o, in_=i)
             else:
                 nc.vector.tensor_copy(out=o, in_=i)
 
-        def uq(c):
-            uc[c], us[c] = quant(ug[c][:].rearrange("p g n -> p (g n)"), "u%d" % c, 2 * CW)
+        def uah(c, g):
+            ub[c, g] = keep.tile([P, 4, P], BF16, name="ub%d%d" % (c, g), align_bytes=A)
+            for t in range(4):
+                nc.scalar.activation(ub[c, g][:, t, :], up[c, g, 1][:, t, :], ACT.Identity, bias=ucols[:, 4 * g + t : 4 * g + t + 1])
+
+        def uih(c, g):
+            nc.scalar.copy(out=get_ug(c, g)[:, 512:1024].rearrange("p (r i t) -> p r t i", i=4, t=4), in_=ub[c, g][:].rearrange("p t (r i) -> p r t i", i=4))
+
+        def uq(c, g=None):
+            if g is None:
+                codes, plane = quant(ug[c][:].rearrange("p g n -> p (g n)"), "u%d" % c, 2 * CW)
+                for k in range(2):
+                    uc[c, k], us[c, k] = codes[:, CW * k : CW * k + CW], plane[:, CW * k : CW * k + CW]
+            else:
+                codes, plane = quant(get_ug(c, g), "u%d%d" % (c, g), CW)
+                uc[c, g], us[c, g] = codes[:], plane[:]
 
         gp, gel, gg, gc, gs = {}, {}, {}, {}, {}
         yt, ygt, yq_ = {}, {}, {}
@@ -278,7 +301,7 @@ def tile_deepinfomaxlocalglobaljsdmap_w8_kernel(
         def gq():
             gc[0], gs[0] = quant(gg[0][:].rearrange("p g n -> p (g n)"), "g", 2 * CW)
 
-        sp, rt, ex, wt = {}, {}, {}, {}
+        sp, rt, ex, at, wt = {}, {}, {}, {}, {}
 
         def smm(c, i):
             h, lp = c // 2, c % 2
@@ -288,155 +311,162 @@ def tile_deepinfomaxlocalglobaljsdmap_w8_kernel(
                 nc.tensor.matmul_mx(
                     out=sp[h, i][:, CW * lp : CW * lp + CW],
                     lhsT=gc[0][:, CW * g + P * i : CW * g + P * i + P].bitcast(X4), lhsT_scale=gs[0][:, CW * g + P * i : CW * g + P * i + P],
-                    rhs=uc[c][:, CW * g : CW * g + CW].bitcast(X4), rhs_scale=us[c][:, CW * g : CW * g + CW],
+                    rhs=uc[c, g].bitcast(X4), rhs_scale=us[c, g],
                     start=(g == 0), stop=(g == 1),
                 )
 
-        def diag(c):
-            h, lp = c // 2, c % 2
-            cs = slice(CW * lp, CW * lp + CW)
-            if h not in rt:
-                rt[h] = keep.tile([P, 512], F32, name="rt%d" % h, align_bytes=A)
-            nc.vector.tensor_tensor(
-                out=rt[h][:, cs].rearrange("p (l j) -> p l j", l=2), in0=sp[h, h][:, cs].rearrange("p (l j) -> p l j", l=2),
-                in1=sgn[:, 2 * lp : 2 * lp + 2, :], op=ALU.mult,
-            )
-
-        def exp(c, i):
+        def tanh(c, i):
             h, lp = c // 2, c % 2
             cs = slice(CW * lp, CW * lp + CW)
             if (h, i) not in ex:
-                ex[h, i] = keep.tile([P, 512], F32, name="ex%d%d" % (h, i), align_bytes=A)
-            src = rt[h][:, cs] if i == h else sp[h, i][:, cs]
-            nc.scalar.activation(ex[h, i][:, cs], src, ACT.Exp)
+                ex[h, i] = keep.tile([P, 512], F32, name="th%d%d" % (h, i), align_bytes=A)
+            nc.scalar.activation(ex[h, i][:, cs], sp[h, i][:, cs], ACT.Tanh, scale=0.5)
 
-        def ln(h, i):
+        def absv(h, i):
+            at[h, i] = keep.tile([P, 512], F32, name="at%d%d" % (h, i), align_bytes=A)
+            nc.vector.scalar_tensor_tensor(out=at[h, i][:], in0=ex[h, i][:], scalar=-1.0, in1=ex[h, i][:], op0=ALU.mult, op1=ALU.max)
+
+        def ln(h, i, parts=1):
             wt[h, i] = keep.tile([P, 512], F32, name="w%d%d" % (h, i), align_bytes=A)
-            nc.scalar.activation(wt[h, i][:], ex[h, i][:], ACT.Ln, bias=1.0)
+            for k in range(parts):
+                js = slice(k * P // parts, (k + 1) * P // parts)
+                nc.scalar.activation(
+                    wt[h, i][:].rearrange("p (l j) -> p l j", l=4)[:, :, js],
+                    at[h, i][:].rearrange("p (l j) -> p l j", l=4)[:, :, js],
+                    ACT.Ln, scale=0.5, bias=half[:],
+                )
 
-        def stt(h, i):
-            o = keep.tile([P, 512], F32, name="o%d%d" % (h, i), align_bytes=A)
+        def rtt(h):
+            rt[h] = keep.tile([P, 512], F32, name="rt%d" % h, align_bytes=A)
+            nc.vector.tensor_tensor(out=rt[h][:], in0=sp[h, h][:], in1=sgn[:].rearrange("p l j -> p (l j)"), op=ALU.mult)
+
+        def stt(h, i, parts=1):
+            o = keep.tile([P, P, 4], F32, name="o%d%d" % (h, i), align_bytes=A)
             r = rt[h] if i == h else sp[h, i]
-            nc.vector.scalar_tensor_tensor(
-                out=o[:].rearrange("p (j l) -> p j l", l=4),
-                in0=wt[h, i][:].rearrange("p (l j) -> p j l", l=4), scalar=44.0,
-                in1=r[:].rearrange("p (l j) -> p j l", l=4), op0=ALU.min, op1=ALU.max,
-            )
-            nc.sync.dma_start(out=out[P * i : P * i + P, P * h : P * h + P, :].rearrange("i j l -> i (j l)"), in_=o[:])
+            for k in range(parts):
+                js = slice(k * P // parts, (k + 1) * P // parts)
+                nc.vector.scalar_tensor_tensor(
+                    out=o[:, js, :],
+                    in0=r[:].rearrange("p (l j) -> p j l", l=4)[:, js, :], scalar=0.0,
+                    in1=wt[h, i][:].rearrange("p (l j) -> p j l", l=4)[:, js, :], op0=ALU.max, op1=ALU.subtract,
+                )
+                nc.sync.dma_start(out=out[P * i : P * i + P, P * h + js.start : P * h + js.stop, :], in_=o[:, js, :])
 
-        cast(0, 0, "V")
         cast(0, 1, "S")
-        xtrn(0, 0)
-        cast(1, 1, "S")
-        xtrn(0, 1)
-        xtt(0)
         cast(1, 0, "S")
+        cast(0, 0, "V")
+        xtrn(0, 0)
+        xtrn(0, 1)
+        warm(2)
+        btru()
+        cast(1, 1, "S")
+        perm(0)
+        bcpu()
+        cast(3, 0, "S")
+        cast(2, 0, "S")
+        xtt(0)
+        xq(0)
         xtrn(1, 0)
         xtrn(1, 1)
-        perm(0)
-        btru()
-        cast(2, 0, "S")
-        xq(0)
-        ytr()
-        bcpu()
+        warm(1)
         xtt(1)
-        cast(2, 1, "S")
-        umm_s(0, 1, 0)
-        umm_v(0, 0, 1)
-        ycp()
-        umm_v(0, 0, 0)
-        perm(1)
-        btrg()
-        uact(0, 1, 0)
-        xtrn(2, 0)
-        xtrn(2, 1)
-        bcpg()
         cast(3, 1, "S")
+        ytr()
+        perm(1)
         umm_s(0, 1, 1)
-        xtt(2)
+        umm_v(0, 0, 0)
+        umm_s(0, 1, 0)
+        ycp()
         uact(0, 1, 1)
-        cast(3, 0, "S")
-        yq()
-        xq(1)
-        gmm(1, 1)
-        xq(2)
-        gmm(1, 0)
-        gelu(1, 1)
         xtrn(3, 0)
-        uil(0, 1, 0, "G")
-        utt(0, 0, 0)
+        cast(2, 1, "S")
         xtrn(3, 1)
-        gelu(1, 0)
-        utt(0, 0, 1)
-        umm_s(1, 1, 0)
-        uil(0, 1, 1, "G")
-        umm_v(1, 0, 0)
+        btrg()
+        xtrn(2, 0)
+        xq(1)
+        yq()
+        utt(0, 0, 0)
+        xtrn(2, 1)
+        uact(0, 1, 0)
+        bcpg()
         xtt(3)
-        uact(1, 1, 0)
-        gmm(0, 0)
-        gmul(1, 0, "G")
-        umm_v(2, 0, 0)
-        gelu(0, 0)
-        gmm(0, 1)
-        utt(1, 0, 0)
-        gmul(1, 1, "G")
-        gelu(0, 1)
+        uil(0, 1, "S")
         umm_s(1, 1, 1)
-        utt(2, 0, 0)
-        umm_v(2, 0, 1)
-        uact(1, 1, 1)
-        umm_s(2, 1, 1)
-        utt(2, 0, 1)
-        umm_v(1, 0, 1)
-        gmul(0, 0, "G")
-        uact(2, 1, 1)
-        umm_s(2, 1, 0)
-        utt(1, 0, 1)
-        uil(1, 1, 1, "S")
+        xtt(2)
+        umm_s(1, 1, 0)
         xq(3)
+        umm_v(0, 0, 1)
+        utt(0, 0, 1)
+        uact(1, 1, 1)
+        uact(1, 1, 0)
+        umm_v(1, 0, 1)
+        gmm(0, 0)
+        gmm(0, 1)
+        gelu(0, 0)
+        xq(2)
+        gelu(0, 1)
+        umm_v(1, 0, 0)
         uq(0)
-        umm_v(3, 1, 1)
-        uact(2, 1, 0)
-        umm_v(3, 0, 0)
-        gmul(0, 1, "G")
-        utt(3, 1, 1)
-        uil(1, 1, 0, "S")
-        utt(3, 0, 0)
+        utt(1, 0, 1)
+        uil(1, 1, "S")
+        gmm(1, 0)
+        utt(1, 0, 0)
         umm_v(3, 1, 0)
-        uil(2, 1, 1, "G")
+        gmul(0, 1, "V")
+        gmm(1, 1)
+        gelu(1, 0)
         utt(3, 1, 0)
-        umm_v(3, 0, 1)
-        gq()
-        uil(2, 1, 0, "G")
-        utt(3, 0, 1)
-        smm(0, 1)
-        smm(0, 0)
-        exp(0, 1)
+        umm_v(3, 0, 0)
+        umm_v(3, 1, 1)
+        gmul(0, 0, "V")
         uq(1)
-        uq(2)
-        smm(1, 0)
+        umm_s(2, 1, 1)
+        gelu(1, 1)
+        umm_s(2, 1, 0)
+        utt(3, 0, 0)
+        uah(3, 1)
+        uact(2, 1, 1)
+        gmul(1, 1, "V")
+        umm_v(2, 0, 1)
+        uact(2, 1, 0)
+        umm_v(2, 0, 0)
+        gmul(1, 0, "V")
+        utt(2, 0, 1)
+        gq()
+        utt(2, 0, 0)
+        uil(2, 1, "S")
+        umm_v(3, 0, 1)
+        smm(0, 1)
         smm(1, 1)
-        uq(3)
-        smm(2, 0)
+        utt(3, 0, 1)
+        uq(2)
+        smm(0, 0)
+        uih(3, 1)
+        smm(1, 0)
+        tanh(0, 1)
         smm(2, 1)
-        exp(2, 0)
-        diag(0)
+        uq(3)
+        tanh(0, 0)
+        rtt(0)
+        tanh(1, 1)
+        tanh(1, 0)
+        smm(2, 0)
+        tanh(2, 1)
+        tanh(2, 0)
         smm(3, 1)
-        exp(1, 1)
+        absv(0, 0)
         smm(3, 0)
-        diag(2)
-        exp(0, 0)
-        diag(3)
-        exp(2, 1)
-        diag(1)
-        exp(3, 0)
-        exp(3, 1)
-        exp(1, 0)
+        tanh(3, 1)
+        tanh(3, 0)
+        rtt(1)
+        absv(0, 1)
+        absv(1, 0)
+        absv(1, 1)
         ln(0, 0)
-        ln(1, 1)
         stt(0, 0)
-        ln(1, 0)
+        ln(1, 1)
         stt(1, 1)
-        ln(0, 1)
+        ln(1, 0)
         stt(1, 0)
-        stt(0, 1)
+        ln(0, 1, 2)
+        stt(0, 1, 2)

@@ -30,9 +30,8 @@ def tile_deepinfomaxlocalglobaljsdmap_w8_kernel(
         keep = ctx.enter_context(tc.tile_pool(name="keep", bufs=1))
         stage = ctx.enter_context(tc.tile_pool(name="stage", bufs=3))
         ps_tr = ctx.enter_context(tc.psum_pool(name="ps_tr", bufs=2))
-        ps_a = ctx.enter_context(tc.psum_pool(name="ps_a", bufs=2))
-        ps_b = ctx.enter_context(tc.psum_pool(name="ps_b", bufs=2))
-        ps_s = ctx.enter_context(tc.psum_pool(name="ps_s", bufs=2))
+        ps_a = ctx.enter_context(tc.psum_pool(name="ps_a", bufs=3))
+        ps_b = ctx.enter_context(tc.psum_pool(name="ps_b", bufs=3))
         ctx.enter_context(tc.manual_schedule())
 
         xb0 = [keep.tile([P, 2, D], U8, name="xb%d" % c, align_bytes=A) for c in range(2)]
@@ -306,7 +305,7 @@ def tile_deepinfomaxlocalglobaljsdmap_w8_kernel(
         def smm(c, i):
             h, lp = c // 2, c % 2
             if lp == 0:
-                sp[h, i] = ps_s.tile([P, 512], F32, name="s") if h == 0 else ps_tr.tile([P, 512], F32, name="tr")
+                sp[h, i] = ps_tr.tile([P, 512], F32, name="tr") if h == 0 else ps_a.tile([P, 512], F32, name="pa")
             for g in range(2):
                 nc.tensor.matmul_mx(
                     out=sp[h, i][:, CW * lp : CW * lp + CW],
@@ -356,117 +355,118 @@ def tile_deepinfomaxlocalglobaljsdmap_w8_kernel(
         cast(1, 0, "S")
         cast(0, 0, "V")
         xtrn(0, 0)
+        perm(0)
         xtrn(0, 1)
         warm(2)
         btru()
-        cast(1, 1, "S")
-        perm(0)
-        bcpu()
-        cast(3, 0, "S")
-        cast(2, 0, "S")
-        xtt(0)
-        xq(0)
         xtrn(1, 0)
+        cast(1, 1, "S")
         xtrn(1, 1)
         warm(1)
-        xtt(1)
-        cast(3, 1, "S")
+        xtt(0)
         ytr()
-        perm(1)
-        umm_s(0, 1, 1)
-        umm_v(0, 0, 0)
+        bcpu()
+        cast(3, 1, "S")
+        xq(0)
+        cast(3, 0, "S")
         umm_s(0, 1, 0)
-        ycp()
-        uact(0, 1, 1)
-        xtrn(3, 0)
         cast(2, 1, "S")
+        umm_s(0, 1, 1)
+        ycp()
+        cast(2, 0, "S")
+        uact(0, 1, 0)
+        xtt(1)
+        perm(1)
+        umm_v(0, 0, 1)
+        xq(1)
+        xtrn(3, 0)
         xtrn(3, 1)
+        uact(0, 1, 1)
+        yq()
         btrg()
         xtrn(2, 0)
-        xq(1)
-        yq()
-        utt(0, 0, 0)
         xtrn(2, 1)
-        uact(0, 1, 0)
-        bcpg()
-        xtt(3)
-        uil(0, 1, "S")
-        umm_s(1, 1, 1)
-        xtt(2)
-        umm_s(1, 1, 0)
-        xq(3)
-        umm_v(0, 0, 1)
         utt(0, 0, 1)
-        uact(1, 1, 1)
-        uact(1, 1, 0)
-        umm_v(1, 0, 1)
         gmm(0, 0)
+        xtt(3)
+        xtt(2)
+        bcpg()
+        umm_v(0, 0, 0)
         gmm(0, 1)
+        uil(0, 1, "S")
         gelu(0, 0)
-        xq(2)
-        gelu(0, 1)
-        umm_v(1, 0, 0)
-        uq(0)
-        utt(1, 0, 1)
-        uil(1, 1, "S")
+        xq(3)
         gmm(1, 0)
-        utt(1, 0, 0)
-        umm_v(3, 1, 0)
-        gmul(0, 1, "V")
         gmm(1, 1)
+        umm_v(1, 0, 1)
+        gelu(0, 1)
+        utt(0, 0, 0)
+        xq(2)
+        uq(0)
         gelu(1, 0)
-        utt(3, 1, 0)
-        umm_v(3, 0, 0)
-        umm_v(3, 1, 1)
+        umm_s(1, 1, 0)
         gmul(0, 0, "V")
-        uq(1)
-        umm_s(2, 1, 1)
         gelu(1, 1)
+        gmul(0, 1, "V")
+        umm_s(1, 1, 1)
         umm_s(2, 1, 0)
-        utt(3, 0, 0)
-        uah(3, 1)
-        uact(2, 1, 1)
-        gmul(1, 1, "V")
-        umm_v(2, 0, 1)
-        uact(2, 1, 0)
         umm_v(2, 0, 0)
+        utt(1, 0, 1)
+        uact(1, 1, 0)
+        umm_s(2, 1, 1)
+        gmul(1, 1, "V")
+        uact(1, 1, 1)
+        uact(2, 1, 0)
+        umm_v(2, 0, 1)
         gmul(1, 0, "V")
-        utt(2, 0, 1)
-        gq()
+        uact(2, 1, 1)
         utt(2, 0, 0)
+        gq()
+        umm_v(1, 0, 0)
+        utt(2, 0, 1)
+        uil(1, 1, "S")
         uil(2, 1, "S")
         umm_v(3, 0, 1)
+        umm_v(3, 1, 1)
+        utt(1, 0, 0)
+        utt(3, 0, 1)
+        uq(1)
+        umm_v(3, 0, 0)
+        utt(3, 0, 0)
+        smm(0, 0)
+        umm_v(3, 1, 0)
+        uah(3, 1)
+        uih(3, 1)
         smm(0, 1)
         smm(1, 1)
-        utt(3, 0, 1)
         uq(2)
-        smm(0, 0)
-        uih(3, 1)
         smm(1, 0)
-        tanh(0, 1)
+        utt(3, 1, 0)
         smm(2, 1)
-        uq(3)
-        tanh(0, 0)
-        rtt(0)
-        tanh(1, 1)
-        tanh(1, 0)
         smm(2, 0)
-        tanh(2, 1)
-        tanh(2, 0)
-        smm(3, 1)
+        tanh(0, 1)
+        uq(3, 0)
+        tanh(0, 0)
+        tanh(1, 0)
+        tanh(1, 1)
+        uq(3, 1)
         absv(0, 0)
+        tanh(2, 0)
         smm(3, 0)
-        tanh(3, 1)
+        tanh(2, 1)
         tanh(3, 0)
-        rtt(1)
+        smm(3, 1)
+        tanh(3, 1)
         absv(0, 1)
+        rtt(0)
+        rtt(1)
         absv(1, 0)
         absv(1, 1)
         ln(0, 0)
-        stt(0, 0)
-        ln(1, 1)
-        stt(1, 1)
         ln(1, 0)
+        stt(0, 0)
+        ln(0, 1)
         stt(1, 0)
-        ln(0, 1, 2)
-        stt(0, 1, 2)
+        stt(0, 1)
+        ln(1, 1, 2)
+        stt(1, 1, 2)

from contextlib import ExitStack

import concourse.mybir as mybir
from concourse.masks import make_identity

P = 128
B, L, D, E = 256, 4, 512, 1024
FLOPS = 2 * B * L * D * E + 2 * B * D * E + 2 * B * B * L * E

F32 = mybir.dt.float32
BF16 = mybir.dt.bfloat16
I32 = mybir.dt.int32
U32 = mybir.dt.uint32
U8 = mybir.dt.uint8
FP8 = mybir.dt.float8_e4m3fn
X4 = mybir.dt.float8_e4m3fn_x4
ALU = mybir.AluOpType
ACT = mybir.ActivationFunctionType

NC = 4
CW = 256
A = 64


def tile_deepinfomaxlocalglobaljsdmap_w8_kernel(
    tc, x_bytes, x_scale, y, wu_words, wu_scales, bu, wg_words, wg_scales, bg, gain, out
):
    nc = tc.nc
    with ExitStack() as ctx:
        keep = ctx.enter_context(tc.tile_pool(name="keep", bufs=1))
        stage = ctx.enter_context(tc.tile_pool(name="stage", bufs=3))
        ps_tr = ctx.enter_context(tc.psum_pool(name="ps_tr", bufs=2))
        ps_a = ctx.enter_context(tc.psum_pool(name="ps_a", bufs=3))
        ps_b = ctx.enter_context(tc.psum_pool(name="ps_b", bufs=3))
        ctx.enter_context(tc.manual_schedule())

        xb0 = [keep.tile([P, 2, D], U8, name="xb%d" % c, align_bytes=A) for c in range(2)]
        xb1 = keep.tile([P, 4, D], U8, name="xbh", align_bytes=A)
        xsc = keep.tile([P, 4], F32, name="xsc", align_bytes=A)
        yb = keep.tile([P, 2, D], BF16, name="yb", align_bytes=A)
        w_raw = [keep.tile([P, E], I32, name="wraw%d" % w, align_bytes=A) for w in range(2)]
        w_per = [keep.tile([P, E], I32, name="wper%d" % w, align_bytes=A) for w in range(2)]
        sc_raw = [keep.tile([P, E // 4], I32, name="sraw%d" % w, align_bytes=A) for w in range(2)]
        sc_per = [keep.tile([P, E // 4], I32, name="sper%d" % w, align_bytes=A) for w in range(2)]
        rows_u = keep.tile([P, P], BF16, name="rows_u", align_bytes=A)
        rows_g = keep.tile([P, P], BF16, name="rows_g", align_bytes=A)
        ident = keep.tile([P, P], F32, name="ident", align_bytes=A)
        ident_b = keep.tile([P, P], BF16, name="identb", align_bytes=A)
        sgn = keep.tile([P, 4, P], F32, name="sgn", align_bytes=A)
        ucols = keep.tile([P, 8], F32, name="ucols", align_bytes=A)
        bgcols = keep.tile([P, 8], F32, name="bgcols", align_bytes=A)
        gcols = keep.tile([P, 8], F32, name="gcols", align_bytes=A)
        dummy = keep.tile([P, 2], F32, name="dummy", align_bytes=A)

        def load_scales(w, src):
            for q in range(4):
                nc.sync.dma_start(out=sc_raw[w][32 * q : 32 * q + 4, :], in_=src[0, 4 * q : 4 * q + 4, :].bitcast(I32))

        def load_vec(eng, rows, r0, vec):
            eng.dma_start(out=rows[r0 : r0 + 8, :].rearrange("q (b i) -> q b i", i=8), in_=vec.rearrange("(b q i) -> q b i", q=8, i=8))

        def load_w(w, src):
            nc.sync.dma_start(out=w_raw[w][:], in_=src[0].rearrange("p n t -> p (n t)").bitcast(I32))

        nc.vector.memset(sc_raw[0][:], 0)
        nc.vector.memset(rows_u[:], 0.0)
        nc.vector.memset(sc_raw[1][:], 0)
        nc.vector.memset(rows_g[:], 0.0)
        nc.vector.memset(dummy[:], 0.0)
        nc.scalar.activation(dummy[:, 0:1], dummy[:, 1:2], ACT.Gelu)
        nc.sync.dma_start(out=xsc[:], in_=x_scale.rearrange("a b (p t) -> p (a b t)", t=4))
        nc.sync.dma_start(out=xb0[0][:], in_=x_bytes[0:P, 0:2, :])
        load_scales(0, wu_scales)
        load_w(0, wu_words)
        nc.sync.dma_start(out=xb0[1][:], in_=x_bytes[0:P, 2:4, :])
        load_vec(nc.sync, rows_u, 0, bu)
        nc.sync.dma_start(out=xb1[:], in_=x_bytes[P : 2 * P, :, :])
        nc.sync.dma_start(out=yb[:], in_=y.rearrange("(n p) k -> p n k", p=P))
        load_w(1, wg_words)
        load_scales(1, wg_scales)
        load_vec(nc.sync, rows_g, 0, bg)
        load_vec(nc.sync, rows_g, 8, gain)
        make_identity(nc, ident[:])

        def warm(count):
            wps = ps_a.tile([P, 512], F32, name="pa")
            for i in range(count):
                nc.tensor.matmul(wps[:], zeros[:, 0:P], zeros[:], start=True, stop=True)

        zeros = keep.tile([P, 512], BF16, name="zeros", align_bytes=A)
        nc.vector.memset(zeros[:], 0.0)
        half = keep.tile([P, 1], F32, name="half", align_bytes=A)
        nc.vector.memset(half[:], 0.5)
        warm(4)
        nc.vector.tensor_copy(out=ident_b[:], in_=ident[:])
        nc.vector.tensor_scalar(
            out=sgn[:], in0=ident[:].unsqueeze(1).to_broadcast([P, 4, P]), scalar1=-2.0, scalar2=1.0, op0=ALU.mult, op1=ALU.add
        )

        xw, xtr, xg, xc, xs = {}, {}, {}, {}, {}

        def cast(c, n, eng):
            if c not in xw:
                xw[c] = keep.tile([P, 2, D], BF16, name="xw%d" % c, align_bytes=A)
            src = (xb0[c][:, n, :] if c < 2 else xb1[:, 2 * (c - 2) + n, :]).bitcast(FP8)
            if eng == "V":
                nc.vector.tensor_copy(out=xw[c][:, n, :], in_=src)
            elif eng == "G":
                nc.gpsimd.tensor_copy(out=xw[c][:, n, :], in_=src)
            else:
                nc.scalar.copy(out=xw[c][:, n, :], in_=src)

        def transposes(src_tile, tr, n):
            words = src_tile[:, n, :].bitcast(F32)
            for u in range(2):
                nc.tensor.transpose(tr[:, u, P * n : P * n + P], words[:, u : D // 2 : 2], ident[:])

        def xtrn(c, n):
            if n == 0:
                xtr[c] = ps_tr.tile([P, 2, CW], F32, name="tr")
            transposes(xw[c], xtr[c], n)

        def xtt(c):
            xg[c] = keep.tile([P, 4 * CW], BF16, name="xg%d" % c, align_bytes=A)
            flat = xtr[c][:].rearrange("p u r -> p (u r)").bitcast(BF16)
            nc.vector.tensor_tensor(
                out=xg[c][:].rearrange("p (r u e) -> p r u e", u=2, e=2),
                in0=flat.rearrange("p (u r e) -> p r u e", u=2, e=2),
                in1=xsc[:].rearrange("p (u e) -> p u e", u=2).unsqueeze(1).to_broadcast([P, CW, 2, 2]),
                op=ALU.mult,
            )

        def quant(src, name, width):
            codes = keep.tile([P, width], U32, name=name + "c", align_bytes=A)
            plane = keep.tile([P, width], U8, name=name + "s", align_bytes=A)
            nc.vector.quantize_mx(out=codes[:].bitcast(X4), scales=plane[:], in_=src)
            return codes, plane

        def xst():
            xtr["s"] = ps_tr.tile([P, 4, P], F32, name="tr")
            for t in range(4):
                nc.tensor.transpose(xtr["s"][:, t, :], xsc[:, t : t + 1].to_broadcast([P, P]), ident[:])

        def xscp():
            xg["s"] = keep.tile([P, D], F32, name="xsb", align_bytes=A)
            nc.scalar.copy(out=xg["s"][:].rearrange("p (k t) -> p k t", t=4), in_=xtr["s"][:].rearrange("p t k -> p k t"))

        def xtt2(c, n):
            if c not in xw:
                xw[c] = keep.tile([P, 2, D], BF16, name="xw%d" % c, align_bytes=A)
            src = (xb0[c][:, n, :] if c < 2 else xb1[:, 2 * (c - 2) + n, :]).bitcast(FP8)
            nc.vector.tensor_tensor(out=xw[c][:, n, :], in0=src, in1=xg["s"][:], op=ALU.mult)

        def xcp(c):
            xg[c] = keep.tile([P, 4 * CW], BF16, name="xg%d" % c, align_bytes=A)
            nc.scalar.copy(out=xg[c][:].bitcast(F32).rearrange("p (r u) -> p r u", u=2), in_=xtr[c][:].rearrange("p u r -> p r u"))

        def xq(c):
            xc[c], xs[c] = quant(xg[c][:], "x%d" % c, CW)

        def perm(w):
            nc.vector.tensor_copy(
                out=sc_per[w][:].rearrange("p (q b i) -> p q b i", q=8, i=2),
                in_=sc_raw[w][:].rearrange("p (b q i) -> p q b i", q=8, i=2),
            )
            nc.vector.tensor_copy(
                out=w_per[w][:].rearrange("p (q b i) -> p q b i", q=8, i=8),
                in_=w_raw[w][:].rearrange("p (b q i) -> p q b i", q=8, i=8),
            )

        def weights(w, g, t):
            c0 = P * (4 * g + t)
            return w_per[w][:, c0 : c0 + P].bitcast(X4), sc_per[w][:].bitcast(U8)[:, c0 : c0 + P]

        bt = {}

        def btru():
            bt[0] = ps_b.tile([P, P], BF16, name="pb")
            nc.tensor.transpose(bt[0][:], rows_u[:], ident_b[:])

        def bcpu():
            nc.scalar.copy(out=ucols[:], in_=bt[0][:, 0:8])

        def btrg():
            bt[1] = ps_b.tile([P, P], BF16, name="pb")
            nc.tensor.transpose(bt[1][:], rows_g[:], ident_b[:])

        def bcpg():
            nc.scalar.copy(out=bgcols[:], in_=bt[1][:, 0:8])
            nc.scalar.activation(gcols[:], bt[1][:, 8:16], ACT.Copy, scale=0.0625)

        up, ub, ug, uc, us = {}, {}, {}, {}, {}

        def umm_v(c, g, n):
            up[c, g, n] = ps_a.tile([P, 4, P], F32, name="pa")
            for t in range(4):
                lw, ls = weights(0, g, t)
                nc.tensor.matmul_mx(
                    out=up[c, g, n][:, t, :], lhsT=lw, lhsT_scale=ls,
                    rhs=xc[c][:, P * n : P * n + P].bitcast(X4), rhs_scale=xs[c][:, P * n : P * n + P],
                    start=True, stop=True,
                )

        def get_ug(c, g):
            if c not in ug:
                ug[c] = keep.tile([P, 2, 4 * CW], BF16, name="ug%d" % c, align_bytes=A)
            return ug[c][:, g, :]

        def utt(c, g, n):
            nc.vector.tensor_tensor(
                out=get_ug(c, g)[:, 512 * n : 512 * n + 512].rearrange("p (r t) -> p r t", t=4),
                in0=up[c, g, n][:].rearrange("p t r -> p r t"),
                in1=ucols[:, 4 * g : 4 * g + 4].unsqueeze(1).to_broadcast([P, P, 4]),
                op=ALU.add,
            )

        def umm_s(c, g, k):
            up[c, g, k] = ps_b.tile([P, 2, CW], F32, name="pb")
            for j in range(2):
                lw, ls = weights(0, g, 2 * k + j)
                nc.tensor.matmul_mx(
                    out=up[c, g, k][:, j, :], lhsT=lw, lhsT_scale=ls,
                    rhs=xc[c][:].bitcast(X4), rhs_scale=xs[c][:], start=True, stop=True,
                )

        def uact(c, g, k):
            if (c, g) not in ub:
                ub[c, g] = keep.tile([P, 4, CW], BF16, name="ub%d%d" % (c, g), align_bytes=A)
            for j in range(2):
                t = 2 * k + j
                nc.scalar.activation(ub[c, g][:, t, :], up[c, g, k][:, j, :], ACT.Identity, bias=ucols[:, 4 * g + t : 4 * g + t + 1])

        def uil(c, g, eng):
            o = get_ug(c, g).rearrange("p (r i t) -> p r t i", i=4, t=4)
            i = ub[c, g][:].rearrange("p t (r i) -> p r t i", i=4)
            if eng == "S":
                nc.scalar.copy(out=o, in_=i)
            else:
                nc.vector.tensor_copy(out=o, in_=i)

        def uah(c, g):
            ub[c, g] = keep.tile([P, 4, P], BF16, name="ub%d%d" % (c, g), align_bytes=A)
            for t in range(4):
                nc.scalar.activation(ub[c, g][:, t, :], up[c, g, 1][:, t, :], ACT.Identity, bias=ucols[:, 4 * g + t : 4 * g + t + 1])

        def uih(c, g):
            nc.scalar.copy(out=get_ug(c, g)[:, 512:1024].rearrange("p (r i t) -> p r t i", i=4, t=4), in_=ub[c, g][:].rearrange("p t (r i) -> p r t i", i=4))

        def uq(c, g=None):
            if g is None:
                codes, plane = quant(ug[c][:].rearrange("p g n -> p (g n)"), "u%d" % c, 2 * CW)
                for k in range(2):
                    uc[c, k], us[c, k] = codes[:, CW * k : CW * k + CW], plane[:, CW * k : CW * k + CW]
            else:
                codes, plane = quant(get_ug(c, g), "u%d%d" % (c, g), CW)
                uc[c, g], us[c, g] = codes[:], plane[:]

        gp, gel, gg, gc, gs = {}, {}, {}, {}, {}
        yt, ygt, yq_ = {}, {}, {}

        def ytr():
            yt[0] = ps_tr.tile([P, 2, CW], F32, name="tr")
            for n in range(2):
                transposes(yb, yt[0], n)

        def ycp():
            ygt[0] = keep.tile([P, 4 * CW], BF16, name="yg", align_bytes=A)
            nc.scalar.copy(out=ygt[0][:].bitcast(F32).rearrange("p (r u) -> p r u", u=2), in_=yt[0][:].rearrange("p u r -> p r u"))

        def yq():
            yq_[0], yq_[1] = quant(ygt[0][:], "y", CW)

        def gmm(g, k):
            gp[g, k] = ps_b.tile([P, 2, CW], F32, name="pb")
            for j in range(2):
                lw, ls = weights(1, g, 2 * k + j)
                nc.tensor.matmul_mx(
                    out=gp[g, k][:, j, :], lhsT=lw, lhsT_scale=ls,
                    rhs=yq_[0][:].bitcast(X4), rhs_scale=yq_[1][:], start=True, stop=True,
                )

        def gelu(g, k):
            if g not in gel:
                gel[g] = keep.tile([P, 4, CW], F32, name="gel%d" % g, align_bytes=A)
            for j in range(2):
                t = 2 * k + j
                nc.scalar.activation(gel[g][:, t, :], gp[g, k][:, j, :], ACT.Gelu, bias=bgcols[:, 4 * g + t : 4 * g + t + 1])

        def gmul(g, n, eng):
            if 0 not in gg:
                gg[0] = keep.tile([P, 2, 4 * CW], BF16, name="gg", align_bytes=A)
            e = nc.gpsimd if eng == "G" else nc.vector
            e.tensor_tensor(
                out=gg[0][:, g, 512 * n : 512 * n + 512].rearrange("p (r t) -> p r t", t=4),
                in0=gel[g][:, :, P * n : P * n + P].rearrange("p t r -> p r t"),
                in1=gcols[:, 4 * g : 4 * g + 4].unsqueeze(1).to_broadcast([P, P, 4]),
                op=ALU.mult,
            )

        def gq():
            gc[0], gs[0] = quant(gg[0][:].rearrange("p g n -> p (g n)"), "g", 2 * CW)

        sp, rt, ex, at, wt = {}, {}, {}, {}, {}

        def smm(c, i):
            h, lp = c // 2, c % 2
            if lp == 0:
                sp[h, i] = ps_tr.tile([P, 512], F32, name="tr") if h == 0 else ps_a.tile([P, 512], F32, name="pa")
            for g in range(2):
                nc.tensor.matmul_mx(
                    out=sp[h, i][:, CW * lp : CW * lp + CW],
                    lhsT=gc[0][:, CW * g + P * i : CW * g + P * i + P].bitcast(X4), lhsT_scale=gs[0][:, CW * g + P * i : CW * g + P * i + P],
                    rhs=uc[c, g].bitcast(X4), rhs_scale=us[c, g],
                    start=(g == 0), stop=(g == 1),
                )

        def tanh(c, i):
            h, lp = c // 2, c % 2
            cs = slice(CW * lp, CW * lp + CW)
            if (h, i) not in ex:
                ex[h, i] = keep.tile([P, 512], F32, name="th%d%d" % (h, i), align_bytes=A)
            nc.scalar.activation(ex[h, i][:, cs], sp[h, i][:, cs], ACT.Tanh, scale=0.5)

        def absv(h, i):
            at[h, i] = keep.tile([P, 512], F32, name="at%d%d" % (h, i), align_bytes=A)
            nc.vector.scalar_tensor_tensor(out=at[h, i][:], in0=ex[h, i][:], scalar=-1.0, in1=ex[h, i][:], op0=ALU.mult, op1=ALU.max)

        def ln(h, i, parts=1):
            wt[h, i] = keep.tile([P, 512], F32, name="w%d%d" % (h, i), align_bytes=A)
            for k in range(parts):
                js = slice(k * P // parts, (k + 1) * P // parts)
                nc.scalar.activation(
                    wt[h, i][:].rearrange("p (l j) -> p l j", l=4)[:, :, js],
                    at[h, i][:].rearrange("p (l j) -> p l j", l=4)[:, :, js],
                    ACT.Ln, scale=0.5, bias=half[:],
                )

        def rtt(h):
            rt[h] = keep.tile([P, 512], F32, name="rt%d" % h, align_bytes=A)
            nc.vector.tensor_tensor(out=rt[h][:], in0=sp[h, h][:], in1=sgn[:].rearrange("p l j -> p (l j)"), op=ALU.mult)

        def stt(h, i, parts=1):
            o = keep.tile([P, P, 4], F32, name="o%d%d" % (h, i), align_bytes=A)
            r = rt[h] if i == h else sp[h, i]
            for k in range(parts):
                js = slice(k * P // parts, (k + 1) * P // parts)
                nc.vector.scalar_tensor_tensor(
                    out=o[:, js, :],
                    in0=r[:].rearrange("p (l j) -> p j l", l=4)[:, js, :], scalar=0.0,
                    in1=wt[h, i][:].rearrange("p (l j) -> p j l", l=4)[:, js, :], op0=ALU.max, op1=ALU.subtract,
                )
                nc.sync.dma_start(out=out[P * i : P * i + P, P * h + js.start : P * h + js.stop, :], in_=o[:, js, :])

        cast(0, 1, "S")
        cast(1, 0, "S")
        cast(0, 0, "V")
        xtrn(0, 0)
        perm(0)
        xtrn(0, 1)
        warm(2)
        btru()
        xtrn(1, 0)
        cast(1, 1, "S")
        xtrn(1, 1)
        warm(1)
        xtt(0)
        ytr()
        bcpu()
        cast(3, 1, "S")
        xq(0)
        cast(3, 0, "S")
        umm_s(0, 1, 0)
        cast(2, 1, "S")
        umm_s(0, 1, 1)
        ycp()
        cast(2, 0, "S")
        uact(0, 1, 0)
        xtt(1)
        perm(1)
        umm_v(0, 0, 1)
        xq(1)
        xtrn(3, 0)
        xtrn(3, 1)
        uact(0, 1, 1)
        yq()
        btrg()
        xtrn(2, 0)
        xtrn(2, 1)
        utt(0, 0, 1)
        gmm(0, 0)
        xtt(3)
        xtt(2)
        bcpg()
        umm_v(0, 0, 0)
        gmm(0, 1)
        uil(0, 1, "S")
        gelu(0, 0)
        xq(3)
        gmm(1, 0)
        gmm(1, 1)
        umm_v(1, 0, 1)
        gelu(0, 1)
        utt(0, 0, 0)
        xq(2)
        uq(0)
        gelu(1, 0)
        umm_s(1, 1, 0)
        gmul(0, 0, "V")
        gelu(1, 1)
        gmul(0, 1, "V")
        umm_s(1, 1, 1)
        umm_s(2, 1, 0)
        umm_v(2, 0, 0)
        utt(1, 0, 1)
        uact(1, 1, 0)
        umm_s(2, 1, 1)
        gmul(1, 1, "V")
        uact(1, 1, 1)
        uact(2, 1, 0)
        umm_v(2, 0, 1)
        gmul(1, 0, "V")
        uact(2, 1, 1)
        utt(2, 0, 0)
        gq()
        umm_v(1, 0, 0)
        utt(2, 0, 1)
        uil(1, 1, "S")
        uil(2, 1, "S")
        umm_v(3, 0, 1)
        umm_v(3, 1, 1)
        utt(1, 0, 0)
        utt(3, 0, 1)
        uq(1)
        umm_v(3, 0, 0)
        utt(3, 0, 0)
        smm(0, 0)
        umm_v(3, 1, 0)
        uah(3, 1)
        uih(3, 1)
        smm(0, 1)
        smm(1, 1)
        uq(2)
        smm(1, 0)
        utt(3, 1, 0)
        smm(2, 1)
        smm(2, 0)
        tanh(0, 1)
        uq(3, 0)
        tanh(0, 0)
        tanh(1, 0)
        tanh(1, 1)
        uq(3, 1)
        absv(0, 0)
        tanh(2, 0)
        smm(3, 0)
        tanh(2, 1)
        tanh(3, 0)
        smm(3, 1)
        tanh(3, 1)
        absv(0, 1)
        rtt(0)
        rtt(1)
        absv(1, 0)
        absv(1, 1)
        ln(0, 0)
        ln(1, 0)
        stt(0, 0)
        ln(0, 1)
        stt(1, 0)
        stt(0, 1)
        ln(1, 1, 2)
        stt(1, 1, 2)
